import numpy as np
import ml_dtypes


def mxq(x, axis, fmt="e4m3"):
    dtype, down = {"e4m3": (ml_dtypes.float8_e4m3fn, 7), "e5m2": (ml_dtypes.float8_e5m2, 14)}[fmt]
    v = np.moveaxis(np.asarray(x, np.float32).astype(ml_dtypes.bfloat16).astype(np.float64), axis, -1)
    blocks = v.reshape(v.shape[:-1] + (-1, 32))
    amax = np.abs(blocks).max(-1, keepdims=True)
    byte = np.maximum(np.where(amax > 0, np.frexp(amax)[1] - 1 + 127, 0) - down, 1)
    scale = np.exp2(byte - 127.0)
    codes = (blocks / scale).astype(np.float32).astype(dtype).astype(np.float64)
    return np.moveaxis((codes * scale).reshape(v.shape), -1, axis)


WIDE = False


def mx_kscale(k):
    if not WIDE:
        return np.ones(k)
    levels = np.array([10, -10, 5, -5, 0])
    if k % 512:
        return np.exp2(np.random.permutation(np.resize(levels, k // 32))).repeat(32)
    a = np.empty((k // 512, 16))
    for p in range(k // 512):
        a[p, :8] = np.random.permutation(np.resize(levels, 8))
        for g in range(8):
            far = levels[np.abs(levels - a[p, g]) >= 10]
            a[p, g + 8] = far[np.random.randint(len(far))]
    return np.exp2(a.ravel()).repeat(32)


def f64(x):
    return np.asarray(x).astype(np.float64)


def striped(idx):
    return np.tile(idx.reshape(-1, 16).T, (8, 1)).astype(np.uint16)


def unstriped(offs):
    return offs[:16].T.reshape(-1).astype(np.int64)


def pack_weight(w):
    k, n = w.shape
    w = f64(np.asarray(w, np.float32).astype(ml_dtypes.bfloat16)).reshape(k // 32, 32, n)
    amax = np.abs(w).max(1)
    byte = np.clip(np.where(amax > 0, np.frexp(amax)[1] - 1 + 127 - 7, 1), 1, 254)
    scaled = (w * np.exp2(127.0 - byte)[:, None, :]).reshape(k, n).astype(np.float32)
    words = np.ascontiguousarray(scaled.reshape(k // 512, 128, 4, n).transpose(0, 1, 3, 2)).astype(ml_dtypes.float8_e4m3fn).view(np.uint8)
    return words, np.ascontiguousarray(byte.astype(np.uint8).reshape(k // 512, 16, n))


def unpack_weight(words, scales):
    g, p, n, _ = words.shape
    vals = np.ascontiguousarray(words).view(ml_dtypes.float8_e4m3fn).astype(np.float64) * np.repeat(np.exp2(scales.astype(np.float64) - 127.0), 8, axis=1)[..., None]
    return vals.transpose(0, 1, 3, 2).reshape(g * 512, n)


K, T, S, V, N, D = 1024, 1024, 512, 256, 128, 3
P = 2 ** 7


def setup_inputs():
    n = np.random.standard_normal
    s = mx_kscale(K)[:, None]
    packed_xT = pack_weight(n((K, T)) * s)
    return {
        "x_words": packed_xT[0],
        "x_scales": packed_xT[1],
        "w1": (n((K, N)) / np.sqrt(K) / s).astype(np.float32),
        "wgt": (np.tile(np.random.uniform(0.5, 2.0, (D, 1, V)), (1, P, 1))).astype(np.float32),
        "offs": striped(np.random.permutation(T)[:S]),
        "case": striped(np.random.permutation(S)[:V]),
        "pos1": striped(np.random.permutation(S)[:V]),
        "pos2": striped(np.random.permutation(S)[:V]),
        "pos3": striped(np.random.permutation(S)[:V]),
    }


def reference(x_words, x_scales, w1, wgt, offs, case, pos1, pos2, pos3):
    xq = unpack_weight(x_words, x_scales)[:, unstriped(offs)]
    y = mxq(f64(w1), 0, "e4m3").T @ xq
    yc = y[:, unstriped(case)]
    ec = np.exp(yc)
    den = ec + (np.exp(y[:, unstriped(pos1)])) * f64(wgt)[0, :1] + (np.exp(y[:, unstriped(pos2)])) * f64(wgt)[1, :1] + (np.exp(y[:, unstriped(pos3)])) * f64(wgt)[2, :1]
    return ec / den

@@ -1,0 +1,140 @@
+from contextlib import ExitStack
+
+import concourse.mybir as mybir
+
+K, T, S, V, M, D = 1024, 1024, 512, 256, 128, 3
+FLOPS = 2 * K * M * S
+
+F32 = mybir.dt.float32
+BF16 = mybir.dt.bfloat16
+I32 = mybir.dt.int32
+U32 = mybir.dt.uint32
+U16 = mybir.dt.uint16
+U8 = mybir.dt.uint8
+FP8X4 = mybir.dt.float8_e4m3fn_x4
+ACT = mybir.ActivationFunctionType
+ALU = mybir.AluOpType
+
+P = 128
+PACK = 4
+PASSES = 2
+PIECES = ((0, 256), (256, 512))
+HALVES = ((0, 128), (128, 256))
+
+
+def tile_picked_ycox_lik_p_kernel(
+    tc, x_words, x_scales, w1, wgt, offs, case, pos1, pos2, pos3, out
+):
+    nc = tc.nc
+    with ExitStack() as ctx:
+        keep = ctx.enter_context(tc.tile_pool(name="keep", bufs=1))
+        psum = ctx.enter_context(tc.psum_pool(name="psum", bufs=1))
+
+        offs_t = keep.tile([P, S // 16], U16, name="offs_t")
+        nc.sync.dma_start(offs_t[:], offs)
+
+        scale_win = keep.tile([P, T], U8, name="scale_win", align_bytes=64)
+        nc.gpsimd.memset(scale_win[:].bitcast(I32), 0)
+        for q in range(4):
+            nc.scalar.dma_start(
+                scale_win[32 * q : 32 * q + 8, :].bitcast(I32),
+                x_scales[:, 4 * q : 4 * q + 4, :].bitcast(I32),
+            )
+
+        word_win = [keep.tile([P, T], I32, name=f"word_win{o}", align_bytes=64) for o in range(PASSES)]
+        w_raw = [keep.tile([P, PACK, M], F32, name=f"w_raw{o}", align_bytes=64) for o in range(PASSES)]
+
+        def load_words(o):
+            nc.sync.dma_start(word_win[o][:], x_words[o].rearrange("p n t -> p (n t)").bitcast(I32))
+
+        load_words(0)
+        for o in range(PASSES):
+            nc.sync.dma_start(w_raw[o][:], w1[512 * o : 512 * (o + 1), :].rearrange("(p j) m -> p j m", j=PACK))
+        load_words(1)
+
+        pos_t = []
+        for d, pos in enumerate((pos1, pos2, pos3)):
+            t = keep.tile([P, V // 16], U16, name=f"pos_t{d}")
+            nc.sync.dma_start(t[:], pos)
+            pos_t.append(t)
+        case_t = keep.tile([P, V // 16], U16, name="case_t")
+        nc.sync.dma_start(case_t[:], case)
+        wgt_t = keep.tile([P, D, V], F32, name="wgt_t", align_bytes=64)
+        nc.sync.dma_start(wgt_t[:], wgt.rearrange("d p v -> p d v"))
+
+        x_scale = keep.tile([P, S], U8, name="x_scale", align_bytes=64)
+        nc.vector.tensor_copy(x_scale[:], scale_win[:].indirect(offs_t[:]))
+        x_code0 = keep.tile([P, S], U32, name="x_code0", align_bytes=64)
+        nc.vector.tensor_copy(x_code0[:], word_win[0][:].bitcast(U32).indirect(offs_t[:]))
+
+        w_code, w_scale = [], []
+        for o in range(PASSES):
+            grouped = keep.tile([P, M, PACK], BF16, name=f"grouped{o}", tag=f"turn{o}", align_bytes=64)
+            nc.scalar.activation(
+                grouped[:].rearrange("p (c i) t -> p c t i", i=4),
+                w_raw[o][:].rearrange("p t (c i) -> p c t i", i=4),
+                ACT.Copy,
+            )
+            code = keep.tile([P, M], U32, name=f"w_code{o}", align_bytes=64)
+            scale = keep.tile([P, M], U8, name=f"w_scale{o}", align_bytes=64)
+            nc.vector.quantize_mx(
+                out=code[:].bitcast(FP8X4), scales=scale[:], in_=grouped[:].rearrange("p m t -> p (m t)")
+            )
+            w_code.append(code)
+            w_scale.append(scale)
+
+        acc = [psum.tile([P, b - a], F32, name=f"acc{i}") for i, (a, b) in enumerate(PIECES)]
+        for i, (a, b) in enumerate(PIECES):
+            nc.tensor.matmul_mx(
+                out=acc[i][:],
+                lhsT=w_code[0][:].bitcast(FP8X4),
+                lhsT_scale=w_scale[0][:],
+                rhs=x_code0[:, a:b].bitcast(FP8X4),
+                rhs_scale=x_scale[:, a:b],
+                start=True,
+                stop=False,
+            )
+
+        exp_y = keep.tile([P, S], F32, name="exp_y", align_bytes=64)
+        exp_neg = keep.tile([P, S], F32, name="exp_neg", align_bytes=64)
+        for i, (a, b) in enumerate(PIECES):
+            x_code1 = keep.tile([P, b - a], U32, name=f"x_code1_{i}", tag=f"turn{1 - i}", align_bytes=64)
+            nc.vector.tensor_copy(x_code1[:], word_win[1][:].bitcast(U32).indirect(offs_t[:, a // 16 : b // 16]))
+            nc.tensor.matmul_mx(
+                out=acc[i][:],
+                lhsT=w_code[1][:].bitcast(FP8X4),
+                lhsT_scale=w_scale[1][:],
+                rhs=x_code1[:].bitcast(FP8X4),
+                rhs_scale=x_scale[4:128, a:b],
+                start=False,
+                stop=True,
+            )
+            nc.scalar.activation(exp_y[:, a:b], acc[i][:], ACT.Exp)
+        for i, (a, b) in enumerate(PIECES):
+            nc.scalar.activation(exp_neg[:, a:b], acc[i][:], ACT.Exp, scale=-1.0)
+
+        term = [keep.tile([P, V], F32, name=f"term{d}", align_bytes=64) for d in range(D)]
+        pair = keep.tile([P, V], F32, name="pair", align_bytes=64)
+        total = keep.tile([P, V], F32, name="total", align_bytes=64)
+        odds = keep.tile([P, V], F32, name="odds", align_bytes=64)
+        root = keep.tile([P, V], F32, name="root", align_bytes=64)
+        res = keep.tile([P, V], F32, name="res", align_bytes=64)
+
+        def weighted(d, a, b):
+            nc.vector.tensor_tensor(
+                term[d][:, a:b], exp_y[:].indirect(pos_t[d][:, a // 16 : b // 16]), wgt_t[:, d, a:b], ALU.mult
+            )
+
+        weighted(0, 0, V)
+        weighted(1, 0, V)
+        weighted(2, 0, V)
+        nc.vector.tensor_tensor(pair[:], term[0][:], term[1][:], ALU.add)
+        for a, b in HALVES:
+            nc.vector.tensor_tensor(total[:, a:b], pair[:, a:b], term[2][:, a:b], ALU.add)
+        for a, b in HALVES:
+            nc.vector.tensor_tensor(
+                odds[:, a:b], exp_neg[:].indirect(case_t[:, a // 16 : b // 16]), total[:, a:b], ALU.mult
+            )
+            nc.scalar.activation(root[:, a:b], odds[:, a:b], ACT.Abs_reciprocal_sqrt, bias=1.0)
+            nc.scalar.activation(res[:, a:b], root[:, a:b], ACT.Square)
+            nc.sync.dma_start(out[:, a:b], res[:, a:b])

@@ -18,7 +18,7 @@ ALU = mybir.AluOpType
 P = 128
 PACK = 4
 PASSES = 2
-PIECES = ((0, 256), (256, 512))
+PIECES = ((0, 256), (256, 384), (384, 512))
 HALVES = ((0, 128), (128, 256))
 
 
@@ -34,12 +34,7 @@ def tile_picked_ycox_lik_p_kernel(
         nc.sync.dma_start(offs_t[:], offs)
 
         scale_win = keep.tile([P, T], U8, name="scale_win", align_bytes=64)
-        nc.gpsimd.memset(scale_win[:].bitcast(I32), 0)
-        for q in range(4):
-            nc.scalar.dma_start(
-                scale_win[32 * q : 32 * q + 8, :].bitcast(I32),
-                x_scales[:, 4 * q : 4 * q + 4, :].bitcast(I32),
-            )
+        nc.vector.memset(scale_win[:].bitcast(I32), 0)
 
         word_win = [keep.tile([P, T], I32, name=f"word_win{o}", align_bytes=64) for o in range(PASSES)]
         w_raw = [keep.tile([P, PACK, M], F32, name=f"w_raw{o}", align_bytes=64) for o in range(PASSES)]
@@ -48,6 +43,11 @@ def tile_picked_ycox_lik_p_kernel(
             nc.sync.dma_start(word_win[o][:], x_words[o].rearrange("p n t -> p (n t)").bitcast(I32))
 
         load_words(0)
+        for q in range(4):
+            nc.sync.dma_start(
+                scale_win[32 * q : 32 * q + 8, :].bitcast(I32),
+                x_scales[:, 4 * q : 4 * q + 4, :].bitcast(I32),
+            )
         for o in range(PASSES):
             nc.sync.dma_start(w_raw[o][:], w1[512 * o : 512 * (o + 1), :].rearrange("(p j) m -> p j m", j=PACK))
         load_words(1)
@@ -63,11 +63,12 @@ def tile_picked_ycox_lik_p_kernel(
         nc.sync.dma_start(wgt_t[:], wgt.rearrange("d p v -> p d v"))
 
         x_scale = keep.tile([P, S], U8, name="x_scale", align_bytes=64)
-        nc.vector.tensor_copy(x_scale[:], scale_win[:].indirect(offs_t[:]))
         x_code0 = keep.tile([P, S], U32, name="x_code0", align_bytes=64)
         nc.vector.tensor_copy(x_code0[:], word_win[0][:].bitcast(U32).indirect(offs_t[:]))
+        nc.vector.tensor_copy(x_scale[:], scale_win[:].indirect(offs_t[:]))
 
-        w_code, w_scale = [], []
+        w_code = keep.tile([P, PASSES * M], U32, name="w_code", align_bytes=64)
+        w_scale = keep.tile([P, PASSES * M], U8, name="w_scale", align_bytes=64)
         for o in range(PASSES):
             grouped = keep.tile([P, M, PACK], BF16, name=f"grouped{o}", tag=f"turn{o}", align_bytes=64)
             nc.scalar.activation(
@@ -75,36 +76,35 @@ def tile_picked_ycox_lik_p_kernel(
                 w_raw[o][:].rearrange("p t (c i) -> p c t i", i=4),
                 ACT.Copy,
             )
-            code = keep.tile([P, M], U32, name=f"w_code{o}", align_bytes=64)
-            scale = keep.tile([P, M], U8, name=f"w_scale{o}", align_bytes=64)
             nc.vector.quantize_mx(
-                out=code[:].bitcast(FP8X4), scales=scale[:], in_=grouped[:].rearrange("p m t -> p (m t)")
+                out=w_code[:, o * M : (o + 1) * M].bitcast(FP8X4),
+                scales=w_scale[:, o * M : (o + 1) * M],
+                in_=grouped[:].rearrange("p m t -> p (m t)"),
             )
-            w_code.append(code)
-            w_scale.append(scale)
 
         acc = [psum.tile([P, b - a], F32, name=f"acc{i}") for i, (a, b) in enumerate(PIECES)]
         for i, (a, b) in enumerate(PIECES):
             nc.tensor.matmul_mx(
                 out=acc[i][:],
-                lhsT=w_code[0][:].bitcast(FP8X4),
-                lhsT_scale=w_scale[0][:],
+                lhsT=w_code[:, 0:M].bitcast(FP8X4),
+                lhsT_scale=w_scale[:, 0:M],
                 rhs=x_code0[:, a:b].bitcast(FP8X4),
                 rhs_scale=x_scale[:, a:b],
                 start=True,
                 stop=False,
             )
 
+        x_code1 = [keep.tile([P, S // 2], U32, name=f"x_code1_{h}", tag=f"turn{1 - h}", align_bytes=64) for h in range(2)]
         exp_y = keep.tile([P, S], F32, name="exp_y", align_bytes=64)
         exp_neg = keep.tile([P, S], F32, name="exp_neg", align_bytes=64)
         for i, (a, b) in enumerate(PIECES):
-            x_code1 = keep.tile([P, b - a], U32, name=f"x_code1_{i}", tag=f"turn{1 - i}", align_bytes=64)
-            nc.vector.tensor_copy(x_code1[:], word_win[1][:].bitcast(U32).indirect(offs_t[:, a // 16 : b // 16]))
+            picked = x_code1[a // 256][:, a % 256 : a % 256 + b - a]
+            nc.vector.tensor_copy(picked, word_win[1][:].bitcast(U32).indirect(offs_t[:, a // 16 : b // 16]))
             nc.tensor.matmul_mx(
                 out=acc[i][:],
-                lhsT=w_code[1][:].bitcast(FP8X4),
-                lhsT_scale=w_scale[1][:],
-                rhs=x_code1[:].bitcast(FP8X4),
+                lhsT=w_code[:, M : 2 * M].bitcast(FP8X4),
+                lhsT_scale=w_scale[:, M : 2 * M],
+                rhs=picked.bitcast(FP8X4),
                 rhs_scale=x_scale[4:128, a:b],
                 start=False,
                 stop=True,
@@ -136,5 +136,6 @@ def tile_picked_ycox_lik_p_kernel(
                 odds[:, a:b], exp_neg[:].indirect(case_t[:, a // 16 : b // 16]), total[:, a:b], ALU.mult
             )
             nc.scalar.activation(root[:, a:b], odds[:, a:b], ACT.Abs_reciprocal_sqrt, bias=1.0)
-            nc.scalar.activation(res[:, a:b], root[:, a:b], ACT.Square)
+        for a, b in HALVES:
+            nc.vector.tensor_tensor(res[:, a:b], root[:, a:b], root[:, a:b], ALU.mult)
             nc.sync.dma_start(out[:, a:b], res[:, a:b])

@@ -31,7 +31,6 @@ def tile_picked_ycox_lik_p_kernel(
         psum = ctx.enter_context(tc.psum_pool(name="psum", bufs=1))
 
         offs_t = keep.tile([P, S // 16], U16, name="offs_t")
-        nc.sync.dma_start(offs_t[:], offs)
 
         scale_win = keep.tile([P, T], U8, name="scale_win", align_bytes=64)
         nc.vector.memset(scale_win[:].bitcast(I32), 0)
@@ -43,6 +42,7 @@ def tile_picked_ycox_lik_p_kernel(
             nc.sync.dma_start(word_win[o][:], x_words[o].rearrange("p n t -> p (n t)").bitcast(I32))
 
         load_words(0)
+        nc.sync.dma_start(offs_t[:], offs)
         for q in range(4):
             nc.sync.dma_start(
                 scale_win[32 * q : 32 * q + 8, :].bitcast(I32),
@@ -94,11 +94,11 @@ def tile_picked_ycox_lik_p_kernel(
                 stop=False,
             )
 
-        x_code1 = [keep.tile([P, S // 2], U32, name=f"x_code1_{h}", tag=f"turn{1 - h}", align_bytes=64) for h in range(2)]
+        x_code1 = keep.tile([P, S], U32, name="x_code1", tag="turn1", align_bytes=64)
         exp_y = keep.tile([P, S], F32, name="exp_y", align_bytes=64)
         exp_neg = keep.tile([P, S], F32, name="exp_neg", align_bytes=64)
         for i, (a, b) in enumerate(PIECES):
-            picked = x_code1[a // 256][:, a % 256 : a % 256 + b - a]
+            picked = x_code1[:, a:b]
             nc.vector.tensor_copy(picked, word_win[1][:].bitcast(U32).indirect(offs_t[:, a // 16 : b // 16]))
             nc.tensor.matmul_mx(
                 out=acc[i][:],
@@ -118,7 +118,6 @@ def tile_picked_ycox_lik_p_kernel(
         total = keep.tile([P, V], F32, name="total", align_bytes=64)
         odds = keep.tile([P, V], F32, name="odds", align_bytes=64)
         root = keep.tile([P, V], F32, name="root", align_bytes=64)
-        res = keep.tile([P, V], F32, name="res", align_bytes=64)
 
         def weighted(d, a, b):
             nc.vector.tensor_tensor(
@@ -137,5 +136,6 @@ def tile_picked_ycox_lik_p_kernel(
             )
             nc.scalar.activation(root[:, a:b], odds[:, a:b], ACT.Abs_reciprocal_sqrt, bias=1.0)
         for a, b in HALVES:
-            nc.vector.tensor_tensor(res[:, a:b], root[:, a:b], root[:, a:b], ALU.mult)
-            nc.sync.dma_start(out[:, a:b], res[:, a:b])
+            res = total[:, V - b : V - a]
+            nc.vector.tensor_tensor(res, root[:, a:b], root[:, a:b], ALU.mult)
+            nc.sync.dma_start(out[:, a:b], res)

@@ -36,7 +36,7 @@ def tile_picked_ycox_lik_p_kernel(
         nc.vector.memset(scale_win[:].bitcast(I32), 0)
 
         word_win = [keep.tile([P, T], I32, name=f"word_win{o}", align_bytes=64) for o in range(PASSES)]
-        w_raw = [keep.tile([P, PACK, M], F32, name=f"w_raw{o}", align_bytes=64) for o in range(PASSES)]
+        w_raw = [keep.tile([P, PACK, M], F32, name=f"w_raw{o}", tag=f"reuse{o}", align_bytes=64) for o in range(PASSES)]
 
         def load_words(o):
             nc.sync.dma_start(word_win[o][:], x_words[o].rearrange("p n t -> p (n t)").bitcast(I32))
@@ -70,7 +70,7 @@ def tile_picked_ycox_lik_p_kernel(
         w_code = keep.tile([P, PASSES * M], U32, name="w_code", align_bytes=64)
         w_scale = keep.tile([P, PASSES * M], U8, name="w_scale", align_bytes=64)
         for o in range(PASSES):
-            grouped = keep.tile([P, M, PACK], BF16, name=f"grouped{o}", tag=f"turn{o}", align_bytes=64)
+            grouped = keep.tile([P, M, PACK], BF16, name=f"grouped{o}", align_bytes=64)
             nc.scalar.activation(
                 grouped[:].rearrange("p (c i) t -> p c t i", i=4),
                 w_raw[o][:].rearrange("p t (c i) -> p c t i", i=4),
@@ -94,7 +94,7 @@ def tile_picked_ycox_lik_p_kernel(
                 stop=False,
             )
 
-        x_code1 = keep.tile([P, S], U32, name="x_code1", tag="turn1", align_bytes=64)
+        x_code1 = keep.tile([P, S], U32, name="x_code1", tag="reuse1", align_bytes=64)
         exp_y = keep.tile([P, S], F32, name="exp_y", align_bytes=64)
         exp_neg = keep.tile([P, S], F32, name="exp_neg", align_bytes=64)
         for i, (a, b) in enumerate(PIECES):
@@ -126,8 +126,9 @@ def tile_picked_ycox_lik_p_kernel(
 
         weighted(0, 0, V)
         weighted(1, 0, V)
-        weighted(2, 0, V)
+        weighted(2, *HALVES[0])
         nc.vector.tensor_tensor(pair[:], term[0][:], term[1][:], ALU.add)
+        weighted(2, *HALVES[1])
         for a, b in HALVES:
             nc.vector.tensor_tensor(total[:, a:b], pair[:, a:b], term[2][:, a:b], ALU.add)
         for a, b in HALVES:

@@ -126,9 +126,9 @@ def tile_picked_ycox_lik_p_kernel(
 
         weighted(0, 0, V)
         weighted(1, 0, V)
-        weighted(2, *HALVES[0])
-        nc.vector.tensor_tensor(pair[:], term[0][:], term[1][:], ALU.add)
-        weighted(2, *HALVES[1])
+        weighted(2, 0, V)
+        for a, b in HALVES:
+            nc.vector.tensor_tensor(pair[:, a:b], term[0][:, a:b], term[1][:, a:b], ALU.add)
         for a, b in HALVES:
             nc.vector.tensor_tensor(total[:, a:b], pair[:, a:b], term[2][:, a:b], ALU.add)
         for a, b in HALVES:

@@ -20,6 +20,7 @@ PACK = 4
 PASSES = 2
 PIECES = ((0, 256), (256, 384), (384, 512))
 HALVES = ((0, 128), (128, 256))
+THIRDS = ((0, 96), (96, 192), (192, 256))
 
 
 def tile_picked_ycox_lik_p_kernel(
@@ -127,16 +128,17 @@ def tile_picked_ycox_lik_p_kernel(
         weighted(0, 0, V)
         weighted(1, 0, V)
         weighted(2, 0, V)
-        for a, b in HALVES:
+        for a, b in THIRDS:
             nc.vector.tensor_tensor(pair[:, a:b], term[0][:, a:b], term[1][:, a:b], ALU.add)
-        for a, b in HALVES:
+        for a, b in THIRDS:
             nc.vector.tensor_tensor(total[:, a:b], pair[:, a:b], term[2][:, a:b], ALU.add)
-        for a, b in HALVES:
+        for a, b in THIRDS:
             nc.vector.tensor_tensor(
                 odds[:, a:b], exp_neg[:].indirect(case_t[:, a // 16 : b // 16]), total[:, a:b], ALU.mult
             )
             nc.scalar.activation(root[:, a:b], odds[:, a:b], ACT.Abs_reciprocal_sqrt, bias=1.0)
-        for a, b in HALVES:
-            res = total[:, V - b : V - a]
-            nc.vector.tensor_tensor(res, root[:, a:b], root[:, a:b], ALU.mult)
-            nc.sync.dma_start(out[:, a:b], res)
+        res = keep.tile([P, V], F32, name="res", tag="total", align_bytes=64)
+        for a, b in THIRDS:
+            nc.vector.tensor_tensor(res[:, a:b], root[:, a:b], root[:, a:b], ALU.mult)
+        for a, b in ((0, 96), (96, 256)):
+            nc.sync.dma_start(out[:, a:b], res[:, a:b])

@@ -97,7 +97,9 @@ def tile_picked_ycox_lik_p_kernel(
 
         x_code1 = keep.tile([P, S], U32, name="x_code1", tag="reuse1", align_bytes=64)
         exp_y = keep.tile([P, S], F32, name="exp_y", align_bytes=64)
-        exp_neg = keep.tile([P, S], F32, name="exp_neg", align_bytes=64)
+        y_all = keep.tile([P, S], F32, name="y_all", align_bytes=64)
+        minus_one = keep.tile([P, 1], F32, name="minus_one")
+        nc.vector.memset(minus_one[:], -1.0)
         for i, (a, b) in enumerate(PIECES):
             picked = x_code1[:, a:b]
             nc.vector.tensor_copy(picked, word_win[1][:].bitcast(U32).indirect(offs_t[:, a // 16 : b // 16]))
@@ -111,8 +113,13 @@ def tile_picked_ycox_lik_p_kernel(
                 stop=True,
             )
             nc.scalar.activation(exp_y[:, a:b], acc[i][:], ACT.Exp)
-        for i, (a, b) in enumerate(PIECES):
-            nc.scalar.activation(exp_neg[:, a:b], acc[i][:], ACT.Exp, scale=-1.0)
+        for i, (a, b) in enumerate(PIECES[:-1]):
+            nc.vector.tensor_copy(y_all[:, a:b], acc[i][:])
+        nc.scalar.activation(y_all[:, PIECES[-1][0] :], acc[-1][:], ACT.Copy)
+        raw_last = keep.tile([P, V], F32, name="raw_last", align_bytes=64)
+        nc.scalar.activation(raw_last[:], exp_y[:].indirect(pos_t[2][:]), ACT.Copy)
+        inv_case = keep.tile([P, V], F32, name="inv_case", align_bytes=64)
+        nc.scalar.activation(inv_case[:], y_all[:].indirect(case_t[:]), ACT.Exp, scale=minus_one[:])
 
         term = [keep.tile([P, V], F32, name=f"term{d}", align_bytes=64) for d in range(D)]
         pair = keep.tile([P, V], F32, name="pair", align_bytes=64)
@@ -127,15 +134,13 @@ def tile_picked_ycox_lik_p_kernel(
 
         weighted(0, 0, V)
         weighted(1, 0, V)
-        weighted(2, 0, V)
+        nc.vector.tensor_tensor(term[2][:], raw_last[:], wgt_t[:, 2, :], ALU.mult)
         for a, b in THIRDS:
             nc.vector.tensor_tensor(pair[:, a:b], term[0][:, a:b], term[1][:, a:b], ALU.add)
         for a, b in THIRDS:
             nc.vector.tensor_tensor(total[:, a:b], pair[:, a:b], term[2][:, a:b], ALU.add)
         for a, b in THIRDS:
-            nc.vector.tensor_tensor(
-                odds[:, a:b], exp_neg[:].indirect(case_t[:, a // 16 : b // 16]), total[:, a:b], ALU.mult
-            )
+            nc.vector.tensor_tensor(odds[:, a:b], inv_case[:, a:b], total[:, a:b], ALU.mult)
             nc.scalar.activation(root[:, a:b], odds[:, a:b], ACT.Abs_reciprocal_sqrt, bias=1.0)
         res = keep.tile([P, V], F32, name="res", tag="total", align_bytes=64)
         for a, b in THIRDS:

@@ -113,9 +113,8 @@ def tile_picked_ycox_lik_p_kernel(
                 stop=True,
             )
             nc.scalar.activation(exp_y[:, a:b], acc[i][:], ACT.Exp)
-        for i, (a, b) in enumerate(PIECES[:-1]):
+        for i, (a, b) in enumerate(PIECES):
             nc.vector.tensor_copy(y_all[:, a:b], acc[i][:])
-        nc.scalar.activation(y_all[:, PIECES[-1][0] :], acc[-1][:], ACT.Copy)
         raw_last = keep.tile([P, V], F32, name="raw_last", align_bytes=64)
         nc.scalar.activation(raw_last[:], exp_y[:].indirect(pos_t[2][:]), ACT.Copy)
         inv_case = keep.tile([P, V], F32, name="inv_case", align_bytes=64)
@@ -141,9 +140,9 @@ def tile_picked_ycox_lik_p_kernel(
             nc.vector.tensor_tensor(total[:, a:b], pair[:, a:b], term[2][:, a:b], ALU.add)
         for a, b in THIRDS:
             nc.vector.tensor_tensor(odds[:, a:b], inv_case[:, a:b], total[:, a:b], ALU.mult)
-            nc.scalar.activation(root[:, a:b], odds[:, a:b], ACT.Abs_reciprocal_sqrt, bias=1.0)
-        res = keep.tile([P, V], F32, name="res", tag="total", align_bytes=64)
+        res = keep.tile([P, V], F32, name="res", align_bytes=64)
         for a, b in THIRDS:
-            nc.vector.tensor_tensor(res[:, a:b], root[:, a:b], root[:, a:b], ALU.mult)
+            nc.vector.scalar_tensor_tensor(root[:, a:b], odds[:, a:b], 2.0, odds[:, a:b], ALU.add, ALU.mult)
+            nc.scalar.activation(res[:, a:b], root[:, a:b], ACT.Abs_reciprocal_sqrt, bias=1.0)
         for a, b in ((0, 96), (96, 256)):
             nc.sync.dma_start(out[:, a:b], res[:, a:b])

@@ -20,7 +20,7 @@ PACK = 4
 PASSES = 2
 PIECES = ((0, 256), (256, 384), (384, 512))
 HALVES = ((0, 128), (128, 256))
-THIRDS = ((0, 96), (96, 192), (192, 256))
+THIRDS = ((0, 64), (64, 128), (128, 192), (192, 256))
 
 
 def tile_picked_ycox_lik_p_kernel(
@@ -144,5 +144,5 @@ def tile_picked_ycox_lik_p_kernel(
         for a, b in THIRDS:
             nc.vector.scalar_tensor_tensor(root[:, a:b], odds[:, a:b], 2.0, odds[:, a:b], ALU.add, ALU.mult)
             nc.scalar.activation(res[:, a:b], root[:, a:b], ACT.Abs_reciprocal_sqrt, bias=1.0)
-        for a, b in ((0, 96), (96, 256)):
+        for a, b in HALVES:
             nc.sync.dma_start(out[:, a:b], res[:, a:b])

@@ -19,6 +19,7 @@ P = 128
 PACK = 4
 PASSES = 2
 PIECES = ((0, 256), (256, 384), (384, 512))
+SHARE = 64
 HALVES = ((0, 128), (128, 256))
 THIRDS = ((0, 64), (64, 128), (128, 192), (192, 256))
 
@@ -113,10 +114,11 @@ def tile_picked_ycox_lik_p_kernel(
                 stop=True,
             )
             nc.scalar.activation(exp_y[:, a:b], acc[i][:], ACT.Exp)
-        for i, (a, b) in enumerate(PIECES):
+        for i, (a, b) in enumerate(PIECES[:-1]):
             nc.vector.tensor_copy(y_all[:, a:b], acc[i][:])
-        raw_last = keep.tile([P, V], F32, name="raw_last", align_bytes=64)
-        nc.scalar.activation(raw_last[:], exp_y[:].indirect(pos_t[2][:]), ACT.Copy)
+        nc.scalar.activation(y_all[:, PIECES[-1][0] :], acc[-1][:], ACT.Copy)
+        raw_last = keep.tile([P, V - SHARE], F32, name="raw_last", align_bytes=64)
+        nc.scalar.activation(raw_last[:], exp_y[:].indirect(pos_t[2][:, SHARE // 16 :]), ACT.Copy)
         inv_case = keep.tile([P, V], F32, name="inv_case", align_bytes=64)
         nc.scalar.activation(inv_case[:], y_all[:].indirect(case_t[:]), ACT.Exp, scale=minus_one[:])
 
@@ -133,7 +135,8 @@ def tile_picked_ycox_lik_p_kernel(
 
         weighted(0, 0, V)
         weighted(1, 0, V)
-        nc.vector.tensor_tensor(term[2][:], raw_last[:], wgt_t[:, 2, :], ALU.mult)
+        weighted(2, 0, SHARE)
+        nc.vector.tensor_tensor(term[2][:, SHARE:], raw_last[:], wgt_t[:, 2, SHARE:], ALU.mult)
         for a, b in THIRDS:
             nc.vector.tensor_tensor(pair[:, a:b], term[0][:, a:b], term[1][:, a:b], ALU.add)
         for a, b in THIRDS:

@@ -19,7 +19,7 @@ P = 128
 PACK = 4
 PASSES = 2
 PIECES = ((0, 256), (256, 384), (384, 512))
-SHARE = 64
+SHARE = 128
 HALVES = ((0, 128), (128, 256))
 THIRDS = ((0, 64), (64, 128), (128, 192), (192, 256))
 
@@ -143,9 +143,9 @@ def tile_picked_ycox_lik_p_kernel(
             nc.vector.tensor_tensor(total[:, a:b], pair[:, a:b], term[2][:, a:b], ALU.add)
         for a, b in THIRDS:
             nc.vector.tensor_tensor(odds[:, a:b], inv_case[:, a:b], total[:, a:b], ALU.mult)
+            nc.scalar.activation(root[:, a:b], odds[:, a:b], ACT.Abs_reciprocal_sqrt, bias=1.0)
         res = keep.tile([P, V], F32, name="res", align_bytes=64)
         for a, b in THIRDS:
-            nc.vector.scalar_tensor_tensor(root[:, a:b], odds[:, a:b], 2.0, odds[:, a:b], ALU.add, ALU.mult)
-            nc.scalar.activation(res[:, a:b], root[:, a:b], ACT.Abs_reciprocal_sqrt, bias=1.0)
+            nc.vector.tensor_tensor(res[:, a:b], root[:, a:b], root[:, a:b], ALU.mult)
         for a, b in HALVES:
             nc.sync.dma_start(out[:, a:b], res[:, a:b])

@@ -30,6 +30,7 @@ def tile_picked_ycox_lik_p_kernel(
     nc = tc.nc
     with ExitStack() as ctx:
         keep = ctx.enter_context(tc.tile_pool(name="keep", bufs=1))
+        shared = ctx.enter_context(tc.tile_pool(name="shared", bufs=1))
         psum = ctx.enter_context(tc.psum_pool(name="psum", bufs=1))
 
         offs_t = keep.tile([P, S // 16], U16, name="offs_t")
@@ -38,7 +39,7 @@ def tile_picked_ycox_lik_p_kernel(
         nc.vector.memset(scale_win[:].bitcast(I32), 0)
 
         word_win = [keep.tile([P, T], I32, name=f"word_win{o}", align_bytes=64) for o in range(PASSES)]
-        w_raw = [keep.tile([P, PACK, M], F32, name=f"w_raw{o}", tag=f"reuse{o}", align_bytes=64) for o in range(PASSES)]
+        w_raw = [shared.tile([P, PACK, M], F32, name=f"w_raw{o}", align_bytes=64, offset=2048 * o) for o in range(PASSES)]
 
         def load_words(o):
             nc.sync.dma_start(word_win[o][:], x_words[o].rearrange("p n t -> p (n t)").bitcast(I32))
@@ -61,8 +62,6 @@ def tile_picked_ycox_lik_p_kernel(
             pos_t.append(t)
         case_t = keep.tile([P, V // 16], U16, name="case_t")
         nc.sync.dma_start(case_t[:], case)
-        wgt_t = keep.tile([P, D, V], F32, name="wgt_t", align_bytes=64)
-        nc.sync.dma_start(wgt_t[:], wgt.rearrange("d p v -> p d v"))
 
         x_scale = keep.tile([P, S], U8, name="x_scale", align_bytes=64)
         x_code0 = keep.tile([P, S], U32, name="x_code0", align_bytes=64)
@@ -84,6 +83,9 @@ def tile_picked_ycox_lik_p_kernel(
                 in_=grouped[:].rearrange("p m t -> p (m t)"),
             )
 
+        wgt_t = shared.tile([P, D, V], F32, name="wgt_t", align_bytes=64, offset=0)
+        nc.sync.dma_start(wgt_t[:], wgt.rearrange("d p v -> p d v"))
+
         acc = [psum.tile([P, b - a], F32, name=f"acc{i}") for i, (a, b) in enumerate(PIECES)]
         for i, (a, b) in enumerate(PIECES):
             nc.tensor.matmul_mx(
@@ -96,7 +98,7 @@ def tile_picked_ycox_lik_p_kernel(
                 stop=False,
             )
 
-        x_code1 = keep.tile([P, S], U32, name="x_code1", tag="reuse1", align_bytes=64)
+        x_code1 = shared.tile([P, S], U32, name="x_code1", align_bytes=64, offset=3072)
         exp_y = keep.tile([P, S], F32, name="exp_y", align_bytes=64)
         y_all = keep.tile([P, S], F32, name="y_all", align_bytes=64)
         minus_one = keep.tile([P, 1], F32, name="minus_one")

@@ -35,11 +35,11 @@ def tile_picked_ycox_lik_p_kernel(
 
         offs_t = keep.tile([P, S // 16], U16, name="offs_t")
 
-        scale_win = keep.tile([P, T], U8, name="scale_win", align_bytes=64)
+        scale_win = keep.tile([P, T], U8, name="scale_win", align_bytes=256)
         nc.vector.memset(scale_win[:].bitcast(I32), 0)
 
-        word_win = [keep.tile([P, T], I32, name=f"word_win{o}", align_bytes=64) for o in range(PASSES)]
-        w_raw = [shared.tile([P, PACK, M], F32, name=f"w_raw{o}", align_bytes=64, offset=2048 * o) for o in range(PASSES)]
+        word_win = [keep.tile([P, T], I32, name=f"word_win{o}", align_bytes=256) for o in range(PASSES)]
+        w_raw = [shared.tile([P, PACK, M], F32, name=f"w_raw{o}", align_bytes=256, offset=2048 * o) for o in range(PASSES)]
 
         def load_words(o):
             nc.sync.dma_start(word_win[o][:], x_words[o].rearrange("p n t -> p (n t)").bitcast(I32))
@@ -63,15 +63,15 @@ def tile_picked_ycox_lik_p_kernel(
         case_t = keep.tile([P, V // 16], U16, name="case_t")
         nc.sync.dma_start(case_t[:], case)
 
-        x_scale = keep.tile([P, S], U8, name="x_scale", align_bytes=64)
-        x_code0 = keep.tile([P, S], U32, name="x_code0", align_bytes=64)
+        x_scale = keep.tile([P, S], U8, name="x_scale", align_bytes=256)
+        x_code0 = keep.tile([P, S], U32, name="x_code0", align_bytes=256)
         nc.vector.tensor_copy(x_code0[:], word_win[0][:].bitcast(U32).indirect(offs_t[:]))
         nc.vector.tensor_copy(x_scale[:], scale_win[:].indirect(offs_t[:]))
 
-        w_code = keep.tile([P, PASSES * M], U32, name="w_code", align_bytes=64)
-        w_scale = keep.tile([P, PASSES * M], U8, name="w_scale", align_bytes=64)
+        w_code = keep.tile([P, PASSES * M], U32, name="w_code", align_bytes=256)
+        w_scale = keep.tile([P, PASSES * M], U8, name="w_scale", align_bytes=256)
         for o in range(PASSES):
-            grouped = keep.tile([P, M, PACK], BF16, name=f"grouped{o}", align_bytes=64)
+            grouped = keep.tile([P, M, PACK], BF16, name=f"grouped{o}", align_bytes=256)
             nc.scalar.activation(
                 grouped[:].rearrange("p (c i) t -> p c t i", i=4),
                 w_raw[o][:].rearrange("p t (c i) -> p c t i", i=4),
@@ -83,7 +83,7 @@ def tile_picked_ycox_lik_p_kernel(
                 in_=grouped[:].rearrange("p m t -> p (m t)"),
             )
 
-        wgt_t = shared.tile([P, D, V], F32, name="wgt_t", align_bytes=64, offset=0)
+        wgt_t = shared.tile([P, D, V], F32, name="wgt_t", align_bytes=256, offset=0)
         nc.sync.dma_start(wgt_t[:], wgt.rearrange("d p v -> p d v"))
 
         acc = [psum.tile([P, b - a], F32, name=f"acc{i}") for i, (a, b) in enumerate(PIECES)]
@@ -98,9 +98,9 @@ def tile_picked_ycox_lik_p_kernel(
                 stop=False,
             )
 
-        x_code1 = shared.tile([P, S], U32, name="x_code1", align_bytes=64, offset=3072)
-        exp_y = keep.tile([P, S], F32, name="exp_y", align_bytes=64)
-        y_all = keep.tile([P, S], F32, name="y_all", align_bytes=64)
+        x_code1 = shared.tile([P, S], U32, name="x_code1", align_bytes=256, offset=3072)
+        exp_y = keep.tile([P, S], F32, name="exp_y", align_bytes=256)
+        y_all = keep.tile([P, S], F32, name="y_all", align_bytes=256)
         minus_one = keep.tile([P, 1], F32, name="minus_one")
         nc.vector.memset(minus_one[:], -1.0)
         for i, (a, b) in enumerate(PIECES):
@@ -119,16 +119,16 @@ def tile_picked_ycox_lik_p_kernel(
         for i, (a, b) in enumerate(PIECES[:-1]):
             nc.vector.tensor_copy(y_all[:, a:b], acc[i][:])
         nc.scalar.activation(y_all[:, PIECES[-1][0] :], acc[-1][:], ACT.Copy)
-        raw_last = keep.tile([P, V - SHARE], F32, name="raw_last", align_bytes=64)
+        raw_last = keep.tile([P, V - SHARE], F32, name="raw_last", align_bytes=256)
         nc.scalar.activation(raw_last[:], exp_y[:].indirect(pos_t[2][:, SHARE // 16 :]), ACT.Copy)
-        inv_case = keep.tile([P, V], F32, name="inv_case", align_bytes=64)
+        inv_case = keep.tile([P, V], F32, name="inv_case", align_bytes=256)
         nc.scalar.activation(inv_case[:], y_all[:].indirect(case_t[:]), ACT.Exp, scale=minus_one[:])
 
-        term = [keep.tile([P, V], F32, name=f"term{d}", align_bytes=64) for d in range(D)]
-        pair = keep.tile([P, V], F32, name="pair", align_bytes=64)
-        total = keep.tile([P, V], F32, name="total", align_bytes=64)
-        odds = keep.tile([P, V], F32, name="odds", align_bytes=64)
-        root = keep.tile([P, V], F32, name="root", align_bytes=64)
+        term = [keep.tile([P, V], F32, name=f"term{d}", align_bytes=256) for d in range(D)]
+        pair = keep.tile([P, V], F32, name="pair", align_bytes=256)
+        total = keep.tile([P, V], F32, name="total", align_bytes=256)
+        odds = keep.tile([P, V], F32, name="odds", align_bytes=256)
+        root = keep.tile([P, V], F32, name="root", align_bytes=256)
 
         def weighted(d, a, b):
             nc.vector.tensor_tensor(
@@ -146,7 +146,7 @@ def tile_picked_ycox_lik_p_kernel(
         for a, b in THIRDS:
             nc.vector.tensor_tensor(odds[:, a:b], inv_case[:, a:b], total[:, a:b], ALU.mult)
             nc.scalar.activation(root[:, a:b], odds[:, a:b], ACT.Abs_reciprocal_sqrt, bias=1.0)
-        res = keep.tile([P, V], F32, name="res", align_bytes=64)
+        res = keep.tile([P, V], F32, name="res", align_bytes=256)
         for a, b in THIRDS:
             nc.vector.tensor_tensor(res[:, a:b], root[:, a:b], root[:, a:b], ALU.mult)
         for a, b in HALVES:

@@ -19,7 +19,7 @@ P = 128
 PACK = 4
 PASSES = 2
 PIECES = ((0, 256), (256, 384), (384, 512))
-SHARE = 128
+SHARE = 96
 HALVES = ((0, 128), (128, 256))
 THIRDS = ((0, 64), (64, 128), (128, 192), (192, 256))
 
@@ -100,7 +100,7 @@ def tile_picked_ycox_lik_p_kernel(
 
         x_code1 = shared.tile([P, S], U32, name="x_code1", align_bytes=256, offset=3072)
         exp_y = keep.tile([P, S], F32, name="exp_y", align_bytes=256)
-        y_all = keep.tile([P, S], F32, name="y_all", align_bytes=256)
+        y_all = shared.tile([P, S], F32, name="y_all", align_bytes=256, offset=5120)
         minus_one = keep.tile([P, 1], F32, name="minus_one")
         nc.vector.memset(minus_one[:], -1.0)
         for i, (a, b) in enumerate(PIECES):
@@ -125,7 +125,8 @@ def tile_picked_ycox_lik_p_kernel(
         nc.scalar.activation(inv_case[:], y_all[:].indirect(case_t[:]), ACT.Exp, scale=minus_one[:])
 
         term = [keep.tile([P, V], F32, name=f"term{d}", align_bytes=256) for d in range(D)]
-        pair = keep.tile([P, V], F32, name="pair", align_bytes=256)
+        pair = [keep.tile([P, b - a], F32, name=f"pair{i}", align_bytes=256) for i, (a, b) in enumerate(THIRDS[:-1])]
+        pair.append(shared.tile([P, THIRDS[-1][1] - THIRDS[-1][0]], F32, name="pair_last", align_bytes=256, offset=5120))
         total = keep.tile([P, V], F32, name="total", align_bytes=256)
         odds = keep.tile([P, V], F32, name="odds", align_bytes=256)
         root = keep.tile([P, V], F32, name="root", align_bytes=256)
@@ -139,10 +140,10 @@ def tile_picked_ycox_lik_p_kernel(
         weighted(1, 0, V)
         weighted(2, 0, SHARE)
         nc.vector.tensor_tensor(term[2][:, SHARE:], raw_last[:], wgt_t[:, 2, SHARE:], ALU.mult)
-        for a, b in THIRDS:
-            nc.vector.tensor_tensor(pair[:, a:b], term[0][:, a:b], term[1][:, a:b], ALU.add)
-        for a, b in THIRDS:
-            nc.vector.tensor_tensor(total[:, a:b], pair[:, a:b], term[2][:, a:b], ALU.add)
+        for i, (a, b) in enumerate(THIRDS):
+            nc.vector.tensor_tensor(pair[i][:], term[0][:, a:b], term[1][:, a:b], ALU.add)
+        for i, (a, b) in enumerate(THIRDS):
+            nc.vector.tensor_tensor(total[:, a:b], pair[i][:], term[2][:, a:b], ALU.add)
         for a, b in THIRDS:
             nc.vector.tensor_tensor(odds[:, a:b], inv_case[:, a:b], total[:, a:b], ALU.mult)
             nc.scalar.activation(root[:, a:b], odds[:, a:b], ACT.Abs_reciprocal_sqrt, bias=1.0)

@@ -19,7 +19,7 @@ P = 128
 PACK = 4
 PASSES = 2
 PIECES = ((0, 256), (256, 384), (384, 512))
-SHARE = 96
+SHARE = 160
 HALVES = ((0, 128), (128, 256))
 THIRDS = ((0, 64), (64, 128), (128, 192), (192, 256))
 

@@ -18,7 +18,7 @@ ALU = mybir.AluOpType
 P = 128
 PACK = 4
 PASSES = 2
-PIECES = ((0, 256), (256, 384), (384, 512))
+PIECES = ((0, 128), (128, 256), (256, 384), (384, 512))
 SHARE = 160
 HALVES = ((0, 128), (128, 256))
 THIRDS = ((0, 64), (64, 128), (128, 192), (192, 256))
@@ -116,9 +116,10 @@ def tile_picked_ycox_lik_p_kernel(
                 stop=True,
             )
             nc.scalar.activation(exp_y[:, a:b], acc[i][:], ACT.Exp)
-        for i, (a, b) in enumerate(PIECES[:-1]):
+            if i in (0, len(PIECES) - 1):
+                nc.scalar.activation(y_all[:, a:b], acc[i][:], ACT.Copy)
+        for i, (a, b) in list(enumerate(PIECES))[1:-1]:
             nc.vector.tensor_copy(y_all[:, a:b], acc[i][:])
-        nc.scalar.activation(y_all[:, PIECES[-1][0] :], acc[-1][:], ACT.Copy)
         raw_last = keep.tile([P, V - SHARE], F32, name="raw_last", align_bytes=256)
         nc.scalar.activation(raw_last[:], exp_y[:].indirect(pos_t[2][:, SHARE // 16 :]), ACT.Copy)
         inv_case = keep.tile([P, V], F32, name="inv_case", align_bytes=256)

@@ -19,7 +19,7 @@ P = 128
 PACK = 4
 PASSES = 2
 PIECES = ((0, 128), (128, 256), (256, 384), (384, 512))
-SHARE = 160
+SHARE = 192
 HALVES = ((0, 128), (128, 256))
 THIRDS = ((0, 64), (64, 128), (128, 192), (192, 256))
 

from contextlib import ExitStack

import concourse.mybir as mybir

K, T, S, V, M, D = 1024, 1024, 512, 256, 128, 3
FLOPS = 2 * K * M * S

F32 = mybir.dt.float32
BF16 = mybir.dt.bfloat16
I32 = mybir.dt.int32
U32 = mybir.dt.uint32
U16 = mybir.dt.uint16
U8 = mybir.dt.uint8
FP8X4 = mybir.dt.float8_e4m3fn_x4
ACT = mybir.ActivationFunctionType
ALU = mybir.AluOpType

P = 128
PACK = 4
PASSES = 2
PIECES = ((0, 128), (128, 256), (256, 384), (384, 512))
SHARE = 192
HALVES = ((0, 128), (128, 256))
THIRDS = ((0, 64), (64, 128), (128, 192), (192, 256))


def tile_picked_ycox_lik_p_kernel(
    tc, x_words, x_scales, w1, wgt, offs, case, pos1, pos2, pos3, out
):
    nc = tc.nc
    with ExitStack() as ctx:
        keep = ctx.enter_context(tc.tile_pool(name="keep", bufs=1))
        shared = ctx.enter_context(tc.tile_pool(name="shared", bufs=1))
        psum = ctx.enter_context(tc.psum_pool(name="psum", bufs=1))

        offs_t = keep.tile([P, S // 16], U16, name="offs_t")

        scale_win = keep.tile([P, T], U8, name="scale_win", align_bytes=256)
        nc.vector.memset(scale_win[:].bitcast(I32), 0)

        word_win = [keep.tile([P, T], I32, name=f"word_win{o}", align_bytes=256) for o in range(PASSES)]
        w_raw = [shared.tile([P, PACK, M], F32, name=f"w_raw{o}", align_bytes=256, offset=2048 * o) for o in range(PASSES)]

        def load_words(o):
            nc.sync.dma_start(word_win[o][:], x_words[o].rearrange("p n t -> p (n t)").bitcast(I32))

        load_words(0)
        nc.sync.dma_start(offs_t[:], offs)
        for q in range(4):
            nc.sync.dma_start(
                scale_win[32 * q : 32 * q + 8, :].bitcast(I32),
                x_scales[:, 4 * q : 4 * q + 4, :].bitcast(I32),
            )
        for o in range(PASSES):
            nc.sync.dma_start(w_raw[o][:], w1[512 * o : 512 * (o + 1), :].rearrange("(p j) m -> p j m", j=PACK))
        load_words(1)

        pos_t = []
        for d, pos in enumerate((pos1, pos2, pos3)):
            t = keep.tile([P, V // 16], U16, name=f"pos_t{d}")
            nc.sync.dma_start(t[:], pos)
            pos_t.append(t)
        case_t = keep.tile([P, V // 16], U16, name="case_t")
        nc.sync.dma_start(case_t[:], case)

        x_scale = keep.tile([P, S], U8, name="x_scale", align_bytes=256)
        x_code0 = keep.tile([P, S], U32, name="x_code0", align_bytes=256)
        nc.vector.tensor_copy(x_code0[:], word_win[0][:].bitcast(U32).indirect(offs_t[:]))
        nc.vector.tensor_copy(x_scale[:], scale_win[:].indirect(offs_t[:]))

        w_code = keep.tile([P, PASSES * M], U32, name="w_code", align_bytes=256)
        w_scale = keep.tile([P, PASSES * M], U8, name="w_scale", align_bytes=256)
        for o in range(PASSES):
            grouped = keep.tile([P, M, PACK], BF16, name=f"grouped{o}", align_bytes=256)
            nc.scalar.activation(
                grouped[:].rearrange("p (c i) t -> p c t i", i=4),
                w_raw[o][:].rearrange("p t (c i) -> p c t i", i=4),
                ACT.Copy,
            )
            nc.vector.quantize_mx(
                out=w_code[:, o * M : (o + 1) * M].bitcast(FP8X4),
                scales=w_scale[:, o * M : (o + 1) * M],
                in_=grouped[:].rearrange("p m t -> p (m t)"),
            )

        wgt_t = shared.tile([P, D, V], F32, name="wgt_t", align_bytes=256, offset=0)
        nc.sync.dma_start(wgt_t[:], wgt.rearrange("d p v -> p d v"))

        acc = [psum.tile([P, b - a], F32, name=f"acc{i}") for i, (a, b) in enumerate(PIECES)]
        for i, (a, b) in enumerate(PIECES):
            nc.tensor.matmul_mx(
                out=acc[i][:],
                lhsT=w_code[:, 0:M].bitcast(FP8X4),
                lhsT_scale=w_scale[:, 0:M],
                rhs=x_code0[:, a:b].bitcast(FP8X4),
                rhs_scale=x_scale[:, a:b],
                start=True,
                stop=False,
            )

        x_code1 = shared.tile([P, S], U32, name="x_code1", align_bytes=256, offset=3072)
        exp_y = keep.tile([P, S], F32, name="exp_y", align_bytes=256)
        y_all = shared.tile([P, S], F32, name="y_all", align_bytes=256, offset=5120)
        minus_one = keep.tile([P, 1], F32, name="minus_one")
        nc.vector.memset(minus_one[:], -1.0)
        for i, (a, b) in enumerate(PIECES):
            picked = x_code1[:, a:b]
            nc.vector.tensor_copy(picked, word_win[1][:].bitcast(U32).indirect(offs_t[:, a // 16 : b // 16]))
            nc.tensor.matmul_mx(
                out=acc[i][:],
                lhsT=w_code[:, M : 2 * M].bitcast(FP8X4),
                lhsT_scale=w_scale[:, M : 2 * M],
                rhs=picked.bitcast(FP8X4),
                rhs_scale=x_scale[4:128, a:b],
                start=False,
                stop=True,
            )
            nc.scalar.activation(exp_y[:, a:b], acc[i][:], ACT.Exp)
            if i in (0, len(PIECES) - 1):
                nc.scalar.activation(y_all[:, a:b], acc[i][:], ACT.Copy)
        for i, (a, b) in list(enumerate(PIECES))[1:-1]:
            nc.vector.tensor_copy(y_all[:, a:b], acc[i][:])
        raw_last = keep.tile([P, V - SHARE], F32, name="raw_last", align_bytes=256)
        nc.scalar.activation(raw_last[:], exp_y[:].indirect(pos_t[2][:, SHARE // 16 :]), ACT.Copy)
        inv_case = keep.tile([P, V], F32, name="inv_case", align_bytes=256)
        nc.scalar.activation(inv_case[:], y_all[:].indirect(case_t[:]), ACT.Exp, scale=minus_one[:])

        term = [keep.tile([P, V], F32, name=f"term{d}", align_bytes=256) for d in range(D)]
        pair = [keep.tile([P, b - a], F32, name=f"pair{i}", align_bytes=256) for i, (a, b) in enumerate(THIRDS[:-1])]
        pair.append(shared.tile([P, THIRDS[-1][1] - THIRDS[-1][0]], F32, name="pair_last", align_bytes=256, offset=5120))
        total = keep.tile([P, V], F32, name="total", align_bytes=256)
        odds = keep.tile([P, V], F32, name="odds", align_bytes=256)
        root = keep.tile([P, V], F32, name="root", align_bytes=256)

        def weighted(d, a, b):
            nc.vector.tensor_tensor(
                term[d][:, a:b], exp_y[:].indirect(pos_t[d][:, a // 16 : b // 16]), wgt_t[:, d, a:b], ALU.mult
            )

        weighted(0, 0, V)
        weighted(1, 0, V)
        weighted(2, 0, SHARE)
        nc.vector.tensor_tensor(term[2][:, SHARE:], raw_last[:], wgt_t[:, 2, SHARE:], ALU.mult)
        for i, (a, b) in enumerate(THIRDS):
            nc.vector.tensor_tensor(pair[i][:], term[0][:, a:b], term[1][:, a:b], ALU.add)
        for i, (a, b) in enumerate(THIRDS):
            nc.vector.tensor_tensor(total[:, a:b], pair[i][:], term[2][:, a:b], ALU.add)
        for a, b in THIRDS:
            nc.vector.tensor_tensor(odds[:, a:b], inv_case[:, a:b], total[:, a:b], ALU.mult)
            nc.scalar.activation(root[:, a:b], odds[:, a:b], ACT.Abs_reciprocal_sqrt, bias=1.0)
        res = keep.tile([P, V], F32, name="res", align_bytes=256)
        for a, b in THIRDS:
            nc.vector.tensor_tensor(res[:, a:b], root[:, a:b], root[:, a:b], ALU.mult)
        for a, b in HALVES:
            nc.sync.dma_start(out[:, a:b], res[:, a:b])
